import numpy as np
import ml_dtypes


def mxq(x, axis, fmt="e4m3"):
    dtype, down = {"e4m3": (ml_dtypes.float8_e4m3fn, 7), "e5m2": (ml_dtypes.float8_e5m2, 14)}[fmt]
    v = np.moveaxis(np.asarray(x, np.float32).astype(ml_dtypes.bfloat16).astype(np.float64), axis, -1)
    blocks = v.reshape(v.shape[:-1] + (-1, 32))
    amax = np.abs(blocks).max(-1, keepdims=True)
    byte = np.maximum(np.where(amax > 0, np.frexp(amax)[1] - 1 + 127, 0) - down, 1)
    scale = np.exp2(byte - 127.0)
    codes = (blocks / scale).astype(np.float32).astype(dtype).astype(np.float64)
    return np.moveaxis((codes * scale).reshape(v.shape), -1, axis)


WIDE = False


def mx_kscale(k):
    if not WIDE:
        return np.ones(k)
    levels = np.array([10, -10, 5, -5, 0])
    if k % 512:
        return np.exp2(np.random.permutation(np.resize(levels, k // 32))).repeat(32)
    a = np.empty((k // 512, 16))
    for p in range(k // 512):
        a[p, :8] = np.random.permutation(np.resize(levels, 8))
        for g in range(8):
            far = levels[np.abs(levels - a[p, g]) >= 10]
            a[p, g + 8] = far[np.random.randint(len(far))]
    return np.exp2(a.ravel()).repeat(32)


def f64(x):
    return np.asarray(x).astype(np.float64)


def striped8(idx):
    return np.asarray(idx).reshape(8, -1, 16).transpose(0, 2, 1).reshape(128, -1).astype(np.uint16)


def unstriped8(offs):
    return offs.reshape(8, 16, -1).transpose(0, 2, 1).reshape(8, -1).astype(np.int64)


def pick8(x, idx, run):
    r = np.arange(len(x))
    return x[r[:, None], idx[r % (8 * run) // run]]


E2M1 = np.array([0.0, 0.5, 1.0, 1.5, 2.0, 3.0, 4.0, 6.0, -0.0, -0.5, -1.0, -1.5, -2.0, -3.0, -4.0, -6.0])


def pack_weight(w, fmt):
    k, n = w.shape
    w = f64(np.asarray(w, np.float32).astype(ml_dtypes.bfloat16)).reshape(k // 32, 32, n)
    amax = np.abs(w).max(1)
    if fmt == "e4m3":
        byte = np.frexp(amax)[1] - 1 + 127 - 7
    else:
        mant, ex = np.frexp(amax / 6.0)
        byte = np.where(mant > 0.5, ex, ex - 1) + 127
    byte = np.clip(np.where(amax > 0, byte, 1), 1, 254)
    scaled = (w * np.exp2(127.0 - byte)[:, None, :]).reshape(k, n).astype(np.float32)
    by_word = np.ascontiguousarray(scaled.reshape(k // 512, 128, 4, n).transpose(0, 1, 3, 2))
    if fmt == "e4m3":
        words = by_word.astype(ml_dtypes.float8_e4m3fn).view(np.uint8)
    else:
        c = by_word.astype(ml_dtypes.float4_e2m1fn).view(np.uint8) & 0xF
        words = (c[..., 0::2] | (c[..., 1::2] << 4)).reshape(k // 512, 128, 2 * n)
    return np.ascontiguousarray(words), np.ascontiguousarray(byte.astype(np.uint8).reshape(k // 512, 16, n))


def unpack_weight(words, scales, fmt):
    g, _, n = scales.shape
    words = np.ascontiguousarray(words).reshape(g, 128, n, -1)
    if fmt == "e4m3":
        vals = words.view(ml_dtypes.float8_e4m3fn).astype(np.float64)
    else:
        nib = np.empty((g, 128, n, 4), np.uint8)
        nib[..., 0::2] = words & 0xF
        nib[..., 1::2] = words >> 4
        vals = E2M1[nib]
    vals = vals * np.repeat(np.exp2(scales.astype(np.float64) - 127.0), 8, axis=1)[..., None]
    return vals.transpose(0, 1, 3, 2).reshape(g * 512, n)


D, T, I, Q = 512, 1024, 512, 128


def setup_inputs():
    n = np.random.standard_normal
    idx = np.stack([np.random.permutation(T)[:I] for _ in range(8)])
    idx2 = np.stack([np.random.permutation(T)[:I] for _ in range(8)])
    idx3 = np.stack([np.random.permutation(T)[:I] for _ in range(8)])
    fd = mx_kscale(D)
    keysp = pack_weight(n((D, T)) / fd[:, None], "e4m3")
    return {
        "query": (n((D, Q)) * 0.9 / np.sqrt(D) * fd[:, None]).astype(np.float32),
        "keys_words": keysp[0],
        "keys_scales": keysp[1],
        "lam": (np.random.uniform(0.3, 0.9, (Q, 1))).astype(np.float32),
        "bar": (np.random.uniform(0.0, 0.8, (Q, 1))).astype(np.float32),
        "reserve": (np.random.uniform(20.0, 80.0, (Q, 1))).astype(np.float32),
        "old": (np.random.uniform(0.0, 2.0, (Q, T))).astype(np.float32),
        "fade": (np.random.uniform(0.3, 0.9, (Q, 1))).astype(np.float32),
        "offs": striped8(idx),
        "offs2": striped8(idx2),
        "offs3": striped8(idx3),
    }


def reference(query, keys_words, keys_scales, lam, bar, reserve, old, fade, offs, offs2, offs3):
    idx = unstriped8(offs)
    idx2 = unstriped8(offs2)
    idx3 = unstriped8(offs3)
    keysu = unpack_weight(keys_words, keys_scales, "e4m3")
    queryq = mxq(f64(query), 0, "e4m3")
    a = queryq.T @ keysu
    s = pick8(a, idx, 16) + np.maximum(pick8(a, idx2, 16), pick8(a, idx3, 16)) * f64(lam)
    ce = s - np.mean(s, axis=1, keepdims=True)
    sd = np.sqrt(np.mean(np.square(ce), axis=1, keepdims=True) + 0.1)
    p = np.square(np.maximum(ce / sd - f64(bar), 0.0))
    w = p / (np.sum(p, axis=1, keepdims=True) + f64(reserve))
    ws = w * 256.0
    wf = np.zeros((Q, T))
    wf[np.arange(Q)[:, None], idx[np.arange(Q) % 128 // 16]] = ws
    y = f64(old) * f64(fade) + wf
    return y

@@ -1,0 +1,165 @@
+from contextlib import ExitStack
+
+import concourse.mybir as mybir
+
+D, T, I, Q = 512, 1024, 512, 128
+FLOPS = 2 * D * T * Q
+
+F32 = mybir.dt.float32
+BF16 = mybir.dt.bfloat16
+I32 = mybir.dt.int32
+U32 = mybir.dt.uint32
+U16 = mybir.dt.uint16
+U8 = mybir.dt.uint8
+FP8X4 = mybir.dt.float8_e4m3fn_x4
+ALU = mybir.AluOpType
+ACT = mybir.ActivationFunctionType
+
+P = 128
+PACK = 4
+PIECES = 4
+N = T // PIECES
+KEY_LOADS = 2
+HALF = I // 2
+HALF_COLS = HALF // 16
+PASS_WIDTHS = (256, 256, 256, 128, 128)
+SPLIT3 = 384
+SQUARES_ON_SCALAR = 288
+OUT_WIDTHS = (128, 256, 256, 256, 128)
+
+
+def tile_attend_lookahead_outliers_counts_heads_kernel(
+    tc, query, keys_words, keys_scales, lam, bar, reserve, old, fade, offs, offs2, offs3, out
+):
+    nc = tc.nc
+    with ExitStack() as ctx:
+        sb = ctx.enter_context(tc.tile_pool(name="sb", bufs=1))
+        ps = ctx.enter_context(tc.psum_pool(name="ps", bufs=1))
+
+        key_planes = sb.tile([P, N], U8, align_bytes=64)
+
+        q_raw = sb.tile([P, PACK, Q], F32)
+        nc.sync.dma_start(out=q_raw[:], in_=query.rearrange("(p j) q -> p j q", j=PACK))
+
+        for quad in range(4):
+            rows = keys_scales[0, 4 * quad : 4 * quad + 4, :].bitcast(I32)
+            nc.scalar.dma_start(
+                out=key_planes[32 * quad : 32 * quad + 16, :].bitcast(I32),
+                in_=rows.rearrange("j (m c) -> m j c", m=PIECES),
+            )
+
+        words = keys_words[0].rearrange("p n t -> p (n t)").bitcast(I32)
+        width = T // KEY_LOADS
+        key_codes = []
+        for c in range(KEY_LOADS):
+            codes = sb.tile([P, width], U32, name=f"key_codes{c}", align_bytes=64)
+            nc.sync.dma_start(out=codes[:].bitcast(I32), in_=words[:, c * width : (c + 1) * width])
+            key_codes.append(codes)
+
+        lists = []
+        for name, src in (("list3", offs3), ("list2", offs2), ("list1", offs)):
+            tile = sb.tile([P, I // 16], U16, name=name)
+            nc.sync.dma_start(tile[:], src)
+            lists.append(tile)
+        list3, list2, list1 = lists
+
+        cols = []
+        for name, src in (("lam_col", lam), ("bar_col", bar), ("reserve_col", reserve), ("fade_col", fade)):
+            tile = sb.tile([P, 1], F32, name=name)
+            nc.sync.dma_start(out=tile[:], in_=src)
+            cols.append(tile)
+        lam_col, bar_col, reserve_col, fade_col = cols
+
+        old_sb = sb.tile([P, T], F32)
+        nc.sync.dma_start(out=old_sb[:], in_=old)
+
+        placed = sb.tile([P, T], F32)
+        nc.gpsimd.memset(placed[:], 0.0)
+        ones = sb.tile([P, I - SPLIT3], F32)
+        nc.gpsimd.memset(ones[:], 1.0)
+
+        q_grouped = sb.tile([P, Q, PACK], BF16, align_bytes=64)
+        nc.vector.tensor_copy(out=q_grouped[:], in_=q_raw[:].rearrange("p j q -> p q j"))
+        q_codes = sb.tile([P, Q], U32, align_bytes=64)
+        q_plane = sb.tile([P, Q], U8, align_bytes=64)
+        nc.vector.quantize_mx(
+            out=q_codes[:].bitcast(FP8X4), scales=q_plane[:], in_=q_grouped[:].rearrange("p q j -> p (q j)")
+        )
+
+        a = sb.tile([P, T], F32)
+        first = 0
+        for m, n in enumerate(PASS_WIDTHS):
+            bank = ps.tile([P, n], F32, name=f"bank{m}")
+            load, in_load = divmod(first, width)
+            plane, in_plane = divmod(first, N)
+            nc.tensor.matmul_mx(
+                out=bank[:],
+                lhsT=q_codes[:].bitcast(FP8X4),
+                lhsT_scale=q_plane[:],
+                rhs=key_codes[load][:, in_load : in_load + n].bitcast(FP8X4),
+                rhs_scale=key_planes[4 * plane : P, in_plane : in_plane + n],
+                start=True,
+                stop=True,
+            )
+            if m % 2 == 0:
+                nc.scalar.copy(out=a[:, first : first + n], in_=bank[:])
+            else:
+                nc.vector.tensor_copy(out=a[:, first : first + n], in_=bank[:])
+            first += n
+
+        halves = [slice(h * HALF, (h + 1) * HALF) for h in range(2)]
+        entries = [slice(h * HALF_COLS, (h + 1) * HALF_COLS) for h in range(2)]
+        g1 = [sb.tile([P, HALF], F32, name=f"g1_{h}") for h in range(2)]
+        g2 = sb.tile([P, I], F32)
+        g3 = sb.tile([P, I], F32)
+        nc.scalar.activation(g3[:, :SPLIT3], a[:].indirect(list3[:, : SPLIT3 // 16]), ACT.Copy)
+        nc.vector.tensor_copy(g2[:], a[:].indirect(list2[:]))
+        nc.vector.tensor_tensor(g3[:, SPLIT3:], a[:].indirect(list3[:, SPLIT3 // 16 :]), ones[:], ALU.mult)
+        for h in range(2):
+            nc.scalar.activation(g1[h][:], a[:].indirect(list1[:, entries[h]]), ACT.Copy)
+
+        larger = [sb.tile([P, HALF], F32, name=f"larger{h}") for h in range(2)]
+        for h in range(2):
+            nc.vector.tensor_tensor(larger[h][:], g2[:, halves[h]], g3[:, halves[h]], ALU.max)
+        s = sb.tile([P, I], F32)
+        for h in range(2):
+            nc.vector.scalar_tensor_tensor(s[:, halves[h]], larger[h][:], lam_col[:], g1[h][:], ALU.mult, ALU.add)
+        stats = sb.tile([P, 12], F32)
+        for h in range(2):
+            nc.vector.bn_stats(stats[:, 6 * h : 6 * h + 6], s[:, halves[h]])
+        mean_var = sb.tile([P, 2], F32)
+        nc.vector.bn_aggr(mean_var[:], stats[:])
+
+        inv_sd = sb.tile([P, 1], F32)
+        nc.scalar.activation(inv_sd[:], mean_var[:, 1:2], ACT.Abs_reciprocal_sqrt, bias=0.1)
+        shares = (slice(0, SQUARES_ON_SCALAR), slice(SQUARES_ON_SCALAR, I))
+        ce = sb.tile([P, I], F32)
+        for share in shares:
+            nc.vector.tensor_scalar(ce[:, share], s[:, share], mean_var[:, 0:1], None, ALU.subtract)
+        z = sb.tile([P, I], F32)
+        nc.vector.tensor_scalar(z[:, shares[0]], ce[:, shares[0]], inv_sd[:], bar_col[:], ALU.mult, ALU.max)
+        nc.vector.tensor_scalar(z[:, shares[1]], ce[:, shares[1]], inv_sd[:], bar_col[:], ALU.mult, ALU.subtract)
+        p = sb.tile([P, I], F32)
+        sums = sb.tile([P, 2], F32)
+        nc.scalar.activation(
+            p[:, shares[0]], z[:, shares[0]], ACT.Square, bias=bar_col[:], scale=-1.0, accum_out=sums[:, 0:1]
+        )
+        nc.vector.scalar_tensor_tensor(
+            p[:, shares[1]], z[:, shares[1]], 0.0, z[:, shares[1]], ALU.max, ALU.mult, accum_out=sums[:, 1:2]
+        )
+        total = sb.tile([P, 1], F32)
+        nc.vector.tensor_scalar(total[:], sums[:, 0:1], sums[:, 1:2], reserve_col[:], ALU.add, ALU.add)
+        inv_total = sb.tile([P, 1], F32)
+        nc.vector.reciprocal(inv_total[:], total[:])
+        ws = sb.tile([P, I], F32)
+        nc.vector.tensor_scalar(ws[:], p[:], inv_total[:], 256.0, ALU.mult, ALU.mult)
+        nc.vector.tensor_copy(placed[:].indirect(list1[:]), ws[:])
+
+        first = 0
+        for c, n in enumerate(OUT_WIDTHS):
+            span = slice(first, first + n)
+            first += n
+            result = sb.tile([P, n], F32, name=f"result{c}")
+            nc.vector.scalar_tensor_tensor(result[:], old_sb[:, span], fade_col[:], placed[:, span], ALU.mult, ALU.add)
+            queue = nc.sync if c % 2 == 0 else nc.scalar
+            queue.dma_start(out=out[:, span], in_=result[:])

@@ -41,13 +41,6 @@ def tile_attend_lookahead_outliers_counts_heads_kernel(
         q_raw = sb.tile([P, PACK, Q], F32)
         nc.sync.dma_start(out=q_raw[:], in_=query.rearrange("(p j) q -> p j q", j=PACK))
 
-        for quad in range(4):
-            rows = keys_scales[0, 4 * quad : 4 * quad + 4, :].bitcast(I32)
-            nc.scalar.dma_start(
-                out=key_planes[32 * quad : 32 * quad + 16, :].bitcast(I32),
-                in_=rows.rearrange("j (m c) -> m j c", m=PIECES),
-            )
-
         words = keys_words[0].rearrange("p n t -> p (n t)").bitcast(I32)
         width = T // KEY_LOADS
         key_codes = []
@@ -55,13 +48,20 @@ def tile_attend_lookahead_outliers_counts_heads_kernel(
             codes = sb.tile([P, width], U32, name=f"key_codes{c}", align_bytes=64)
             nc.sync.dma_start(out=codes[:].bitcast(I32), in_=words[:, c * width : (c + 1) * width])
             key_codes.append(codes)
+            if c == 0:
+                for quad in range(4):
+                    rows = keys_scales[0, 4 * quad : 4 * quad + 4, :].bitcast(I32)
+                    nc.sync.dma_start(
+                        out=key_planes[32 * quad : 32 * quad + 16, :].bitcast(I32),
+                        in_=rows.rearrange("j (m c) -> m j c", m=PIECES),
+                    )
 
         lists = []
-        for name, src in (("list3", offs3), ("list2", offs2), ("list1", offs)):
+        for name, src in (("list2", offs2), ("list3", offs3), ("list1", offs)):
             tile = sb.tile([P, I // 16], U16, name=name)
             nc.sync.dma_start(tile[:], src)
             lists.append(tile)
-        list3, list2, list1 = lists
+        list2, list3, list1 = lists
 
         cols = []
         for name, src in (("lam_col", lam), ("bar_col", bar), ("reserve_col", reserve), ("fade_col", fade)):
@@ -74,17 +74,22 @@ def tile_attend_lookahead_outliers_counts_heads_kernel(
         nc.sync.dma_start(out=old_sb[:], in_=old)
 
         placed = sb.tile([P, T], F32)
-        nc.gpsimd.memset(placed[:], 0.0)
+        nc.vector.memset(placed[:], 0.0)
         ones = sb.tile([P, I - SPLIT3], F32)
-        nc.gpsimd.memset(ones[:], 1.0)
+        nc.vector.memset(ones[:], 1.0)
 
         q_grouped = sb.tile([P, Q, PACK], BF16, align_bytes=64)
-        nc.vector.tensor_copy(out=q_grouped[:], in_=q_raw[:].rearrange("p j q -> p q j"))
+        q_halves = (slice(0, Q // 2), slice(Q // 2, Q))
+        for rows in q_halves:
+            nc.vector.tensor_copy(out=q_grouped[:, rows, :], in_=q_raw[:, :, rows].rearrange("p j q -> p q j"))
         q_codes = sb.tile([P, Q], U32, align_bytes=64)
         q_plane = sb.tile([P, Q], U8, align_bytes=64)
-        nc.vector.quantize_mx(
-            out=q_codes[:].bitcast(FP8X4), scales=q_plane[:], in_=q_grouped[:].rearrange("p q j -> p (q j)")
-        )
+        for rows in q_halves:
+            nc.vector.quantize_mx(
+                out=q_codes[:, rows].bitcast(FP8X4),
+                scales=q_plane[:, rows],
+                in_=q_grouped[:, rows, :].rearrange("p q j -> p (q j)"),
+            )
 
         a = sb.tile([P, T], F32)
         first = 0

from contextlib import ExitStack

import concourse.mybir as mybir

D, T, I, Q = 512, 1024, 512, 128
FLOPS = 2 * D * T * Q

F32 = mybir.dt.float32
BF16 = mybir.dt.bfloat16
I32 = mybir.dt.int32
U32 = mybir.dt.uint32
U16 = mybir.dt.uint16
U8 = mybir.dt.uint8
FP8X4 = mybir.dt.float8_e4m3fn_x4
ALU = mybir.AluOpType
ACT = mybir.ActivationFunctionType

P = 128
PACK = 4
PIECES = 4
N = T // PIECES
KEY_LOADS = 2
HALF = I // 2
HALF_COLS = HALF // 16
PASS_WIDTHS = (256, 256, 256, 128, 128)
SPLIT3 = 384
SQUARES_ON_SCALAR = 288
OUT_WIDTHS = (128, 256, 256, 256, 128)


def tile_attend_lookahead_outliers_counts_heads_kernel(
    tc, query, keys_words, keys_scales, lam, bar, reserve, old, fade, offs, offs2, offs3, out
):
    nc = tc.nc
    with ExitStack() as ctx:
        sb = ctx.enter_context(tc.tile_pool(name="sb", bufs=1))
        ps = ctx.enter_context(tc.psum_pool(name="ps", bufs=1))

        key_planes = sb.tile([P, N], U8, align_bytes=64)

        q_raw = sb.tile([P, PACK, Q], F32)
        nc.sync.dma_start(out=q_raw[:], in_=query.rearrange("(p j) q -> p j q", j=PACK))

        words = keys_words[0].rearrange("p n t -> p (n t)").bitcast(I32)
        width = T // KEY_LOADS
        key_codes = []
        for c in range(KEY_LOADS):
            codes = sb.tile([P, width], U32, name=f"key_codes{c}", align_bytes=64)
            nc.sync.dma_start(out=codes[:].bitcast(I32), in_=words[:, c * width : (c + 1) * width])
            key_codes.append(codes)
            if c == 0:
                for quad in range(4):
                    rows = keys_scales[0, 4 * quad : 4 * quad + 4, :].bitcast(I32)
                    nc.sync.dma_start(
                        out=key_planes[32 * quad : 32 * quad + 16, :].bitcast(I32),
                        in_=rows.rearrange("j (m c) -> m j c", m=PIECES),
                    )

        lists = []
        for name, src in (("list2", offs2), ("list3", offs3), ("list1", offs)):
            tile = sb.tile([P, I // 16], U16, name=name)
            nc.sync.dma_start(tile[:], src)
            lists.append(tile)
        list2, list3, list1 = lists

        cols = []
        for name, src in (("lam_col", lam), ("bar_col", bar), ("reserve_col", reserve), ("fade_col", fade)):
            tile = sb.tile([P, 1], F32, name=name)
            nc.sync.dma_start(out=tile[:], in_=src)
            cols.append(tile)
        lam_col, bar_col, reserve_col, fade_col = cols

        old_sb = sb.tile([P, T], F32)
        nc.sync.dma_start(out=old_sb[:], in_=old)

        placed = sb.tile([P, T], F32)
        nc.vector.memset(placed[:], 0.0)
        ones = sb.tile([P, I - SPLIT3], F32)
        nc.vector.memset(ones[:], 1.0)

        q_grouped = sb.tile([P, Q, PACK], BF16, align_bytes=64)
        q_halves = (slice(0, Q // 2), slice(Q // 2, Q))
        for rows in q_halves:
            nc.vector.tensor_copy(out=q_grouped[:, rows, :], in_=q_raw[:, :, rows].rearrange("p j q -> p q j"))
        q_codes = sb.tile([P, Q], U32, align_bytes=64)
        q_plane = sb.tile([P, Q], U8, align_bytes=64)
        for rows in q_halves:
            nc.vector.quantize_mx(
                out=q_codes[:, rows].bitcast(FP8X4),
                scales=q_plane[:, rows],
                in_=q_grouped[:, rows, :].rearrange("p q j -> p (q j)"),
            )

        a = sb.tile([P, T], F32)
        first = 0
        for m, n in enumerate(PASS_WIDTHS):
            bank = ps.tile([P, n], F32, name=f"bank{m}")
            load, in_load = divmod(first, width)
            plane, in_plane = divmod(first, N)
            nc.tensor.matmul_mx(
                out=bank[:],
                lhsT=q_codes[:].bitcast(FP8X4),
                lhsT_scale=q_plane[:],
                rhs=key_codes[load][:, in_load : in_load + n].bitcast(FP8X4),
                rhs_scale=key_planes[4 * plane : P, in_plane : in_plane + n],
                start=True,
                stop=True,
            )
            if m % 2 == 0:
                nc.scalar.copy(out=a[:, first : first + n], in_=bank[:])
            else:
                nc.vector.tensor_copy(out=a[:, first : first + n], in_=bank[:])
            first += n

        halves = [slice(h * HALF, (h + 1) * HALF) for h in range(2)]
        entries = [slice(h * HALF_COLS, (h + 1) * HALF_COLS) for h in range(2)]
        g1 = [sb.tile([P, HALF], F32, name=f"g1_{h}") for h in range(2)]
        g2 = sb.tile([P, I], F32)
        g3 = sb.tile([P, I], F32)
        nc.scalar.activation(g3[:, :SPLIT3], a[:].indirect(list3[:, : SPLIT3 // 16]), ACT.Copy)
        nc.vector.tensor_copy(g2[:], a[:].indirect(list2[:]))
        nc.vector.tensor_tensor(g3[:, SPLIT3:], a[:].indirect(list3[:, SPLIT3 // 16 :]), ones[:], ALU.mult)
        for h in range(2):
            nc.scalar.activation(g1[h][:], a[:].indirect(list1[:, entries[h]]), ACT.Copy)

        larger = [sb.tile([P, HALF], F32, name=f"larger{h}") for h in range(2)]
        for h in range(2):
            nc.vector.tensor_tensor(larger[h][:], g2[:, halves[h]], g3[:, halves[h]], ALU.max)
        s = sb.tile([P, I], F32)
        for h in range(2):
            nc.vector.scalar_tensor_tensor(s[:, halves[h]], larger[h][:], lam_col[:], g1[h][:], ALU.mult, ALU.add)
        stats = sb.tile([P, 12], F32)
        for h in range(2):
            nc.vector.bn_stats(stats[:, 6 * h : 6 * h + 6], s[:, halves[h]])
        mean_var = sb.tile([P, 2], F32)
        nc.vector.bn_aggr(mean_var[:], stats[:])

        inv_sd = sb.tile([P, 1], F32)
        nc.scalar.activation(inv_sd[:], mean_var[:, 1:2], ACT.Abs_reciprocal_sqrt, bias=0.1)
        shares = (slice(0, SQUARES_ON_SCALAR), slice(SQUARES_ON_SCALAR, I))
        ce = sb.tile([P, I], F32)
        for share in shares:
            nc.vector.tensor_scalar(ce[:, share], s[:, share], mean_var[:, 0:1], None, ALU.subtract)
        z = sb.tile([P, I], F32)
        nc.vector.tensor_scalar(z[:, shares[0]], ce[:, shares[0]], inv_sd[:], bar_col[:], ALU.mult, ALU.max)
        nc.vector.tensor_scalar(z[:, shares[1]], ce[:, shares[1]], inv_sd[:], bar_col[:], ALU.mult, ALU.subtract)
        p = sb.tile([P, I], F32)
        sums = sb.tile([P, 2], F32)
        nc.scalar.activation(
            p[:, shares[0]], z[:, shares[0]], ACT.Square, bias=bar_col[:], scale=-1.0, accum_out=sums[:, 0:1]
        )
        nc.vector.scalar_tensor_tensor(
            p[:, shares[1]], z[:, shares[1]], 0.0, z[:, shares[1]], ALU.max, ALU.mult, accum_out=sums[:, 1:2]
        )
        total = sb.tile([P, 1], F32)
        nc.vector.tensor_scalar(total[:], sums[:, 0:1], sums[:, 1:2], reserve_col[:], ALU.add, ALU.add)
        inv_total = sb.tile([P, 1], F32)
        nc.vector.reciprocal(inv_total[:], total[:])
        ws = sb.tile([P, I], F32)
        nc.vector.tensor_scalar(ws[:], p[:], inv_total[:], 256.0, ALU.mult, ALU.mult)
        nc.vector.tensor_copy(placed[:].indirect(list1[:]), ws[:])

        first = 0
        for c, n in enumerate(OUT_WIDTHS):
            span = slice(first, first + n)
            first += n
            result = sb.tile([P, n], F32, name=f"result{c}")
            nc.vector.scalar_tensor_tensor(result[:], old_sb[:, span], fade_col[:], placed[:, span], ALU.mult, ALU.add)
            queue = nc.sync if c % 2 == 0 else nc.scalar
            queue.dma_start(out=out[:, span], in_=result[:])
